import numpy as np
import ml_dtypes


def mxq(x, axis, fmt="e4m3"):
    dtype, down = {"e4m3": (ml_dtypes.float8_e4m3fn, 7), "e5m2": (ml_dtypes.float8_e5m2, 14)}[fmt]
    v = np.moveaxis(np.asarray(x, np.float32).astype(ml_dtypes.bfloat16).astype(np.float64), axis, -1)
    blocks = v.reshape(v.shape[:-1] + (-1, 32))
    amax = np.abs(blocks).max(-1, keepdims=True)
    byte = np.maximum(np.where(amax > 0, np.frexp(amax)[1] - 1 + 127, 0) - down, 1)
    scale = np.exp2(byte - 127.0)
    codes = (blocks / scale).astype(np.float32).astype(dtype).astype(np.float64)
    return np.moveaxis((codes * scale).reshape(v.shape), -1, axis)


WIDE = False


def mx_kscale(k):
    if not WIDE:
        return np.ones(k)
    levels = np.array([10, -10, 5, -5, 0])
    if k % 512:
        return np.exp2(np.random.permutation(np.resize(levels, k // 32))).repeat(32)
    a = np.empty((k // 512, 16))
    for p in range(k // 512):
        a[p, :8] = np.random.permutation(np.resize(levels, 8))
        for g in range(8):
            far = levels[np.abs(levels - a[p, g]) >= 10]
            a[p, g + 8] = far[np.random.randint(len(far))]
    return np.exp2(a.ravel()).repeat(32)


def f64(x):
    return np.asarray(x).astype(np.float64)


def striped8(idx):
    return np.asarray(idx).reshape(8, -1, 16).transpose(0, 2, 1).reshape(128, -1).astype(np.uint16)


def unstriped8(offs):
    return offs.reshape(8, 16, -1).transpose(0, 2, 1).reshape(8, -1).astype(np.int64)


def pick8(x, idx, run):
    r = np.arange(len(x))
    return x[r[:, None], idx[r % (8 * run) // run]]


E2M1 = np.array([0.0, 0.5, 1.0, 1.5, 2.0, 3.0, 4.0, 6.0, -0.0, -0.5, -1.0, -1.5, -2.0, -3.0, -4.0, -6.0])


def pack_weight(w, fmt):
    k, n = w.shape
    w = f64(np.asarray(w, np.float32).astype(ml_dtypes.bfloat16)).reshape(k // 32, 32, n)
    amax = np.abs(w).max(1)
    if fmt == "e4m3":
        byte = np.frexp(amax)[1] - 1 + 127 - 7
    else:
        mant, ex = np.frexp(amax / 6.0)
        byte = np.where(mant > 0.5, ex, ex - 1) + 127
    byte = np.clip(np.where(amax > 0, byte, 1), 1, 254)
    scaled = (w * np.exp2(127.0 - byte)[:, None, :]).reshape(k, n).astype(np.float32)
    by_word = np.ascontiguousarray(scaled.reshape(k // 512, 128, 4, n).transpose(0, 1, 3, 2))
    if fmt == "e4m3":
        words = by_word.astype(ml_dtypes.float8_e4m3fn).view(np.uint8)
    else:
        c = by_word.astype(ml_dtypes.float4_e2m1fn).view(np.uint8) & 0xF
        words = (c[..., 0::2] | (c[..., 1::2] << 4)).reshape(k // 512, 128, 2 * n)
    return np.ascontiguousarray(words), np.ascontiguousarray(byte.astype(np.uint8).reshape(k // 512, 16, n))


def unpack_weight(words, scales, fmt):
    g, _, n = scales.shape
    words = np.ascontiguousarray(words).reshape(g, 128, n, -1)
    if fmt == "e4m3":
        vals = words.view(ml_dtypes.float8_e4m3fn).astype(np.float64)
    else:
        nib = np.empty((g, 128, n, 4), np.uint8)
        nib[..., 0::2] = words & 0xF
        nib[..., 1::2] = words >> 4
        vals = E2M1[nib]
    vals = vals * np.repeat(np.exp2(scales.astype(np.float64) - 127.0), 8, axis=1)[..., None]
    return vals.transpose(0, 1, 3, 2).reshape(g * 512, n)


D, T, U, I, Q = 512, 1024, 1024, 512, 128


def setup_inputs():
    n = np.random.standard_normal
    idx = np.stack([np.random.permutation(T)[:I] for _ in range(8)])
    idx2 = np.stack([np.random.permutation(T)[:I] for _ in range(8)])
    idx3 = np.stack([np.random.permutation(U)[:I] for _ in range(8)])
    idx4 = np.stack([np.random.permutation(U)[:I] for _ in range(8)])
    idx5 = np.stack([np.random.permutation(U)[:I] for _ in range(8)])
    fd = mx_kscale(D)
    keysp = pack_weight(n((D, T)) / fd[:, None], "e2m1")
    notesp = pack_weight(n((D, U)) / fd[:, None], "e4m3")
    return {
        "query": (n((D, Q)) * 1.0 / np.sqrt(D) * fd[:, None]).astype(np.float32),
        "keys_words": keysp[0],
        "keys_scales": keysp[1],
        "notes_words": notesp[0],
        "notes_scales": notesp[1],
        "offs": striped8(idx),
        "offs2": striped8(idx2),
        "offs3": striped8(idx3),
        "offs4": striped8(idx4),
        "offs5": striped8(idx5),
    }


def reference(query, keys_words, keys_scales, notes_words, notes_scales, offs, offs2, offs3, offs4, offs5):
    idx = unstriped8(offs)
    idx2 = unstriped8(offs2)
    idx3 = unstriped8(offs3)
    idx4 = unstriped8(offs4)
    idx5 = unstriped8(offs5)
    keysu = unpack_weight(keys_words, keys_scales, "e2m1")
    notesu = unpack_weight(notes_words, notes_scales, "e4m3")
    queryq = mxq(f64(query), 0, "e4m3")
    a = queryq.T @ keysu
    b = queryq.T @ notesu
    w = np.minimum(pick8(a, idx, 16), pick8(a, idx2, 16))
    v = np.minimum(w, pick8(b, idx3, 16))
    f1 = np.zeros((Q, U))
    f1[np.arange(Q)[:, None], idx4[np.arange(Q) % 128 // 16]] = v
    bb = b - f1
    y = pick8(bb, idx5, 16) + w
    return y

@@ -1,0 +1,151 @@
+from contextlib import ExitStack
+
+import concourse.mybir as mybir
+
+D, T, U, I, Q = 512, 1024, 1024, 512, 128
+FLOPS = 2 * D * Q * (T + U)
+
+F32 = mybir.dt.float32
+BF16 = mybir.dt.bfloat16
+I32 = mybir.dt.int32
+U32 = mybir.dt.uint32
+U16 = mybir.dt.uint16
+U8 = mybir.dt.uint8
+FP8X4 = mybir.dt.float8_e4m3fn_x4
+FP4X4 = mybir.dt.float4_e2m1fn_x4
+ALU = mybir.AluOpType
+COPY = mybir.ActivationFunctionType.Copy
+
+P = 128
+PACK = 4
+N = 256
+HALF = I // 2
+PER_COLUMN = 16
+
+
+def tile_attend_weakestlink_two_kernel(
+    tc, query, keys_words, keys_scales, notes_words, notes_scales, offs, offs2, offs3, offs4, offs5, out
+):
+    nc = tc.nc
+    with ExitStack() as ctx:
+        lists = ctx.enter_context(tc.tile_pool(name="lists", bufs=1))
+        sb = ctx.enter_context(tc.tile_pool(name="sb", bufs=1))
+        psum = ctx.enter_context(tc.psum_pool(name="psum", bufs=1))
+
+        key_plane = sb.tile([P, T], U8, name="key_plane", align_bytes=64)
+        note_plane = sb.tile([P, U], U8, name="note_plane", align_bytes=64)
+        f1 = sb.tile([P, U], F32, name="f1", align_bytes=64)
+        nc.vector.memset(key_plane[:, 0 : T // 2].bitcast(I32), 0)
+        nc.gpsimd.memset(key_plane[:, T // 2 : T].bitcast(I32), 0)
+        nc.vector.memset(note_plane[:].bitcast(I32), 0)
+        nc.vector.memset(f1[:], 0.0)
+
+        def load_scales(queue, plane, scales, quadrant):
+            queue.dma_start(
+                out=plane[32 * quadrant : 32 * quadrant + 4, :].bitcast(I32),
+                in_=scales[0, 4 * quadrant : 4 * quadrant + 4, :].bitcast(I32),
+            )
+
+        def load_list(name, source):
+            tile = lists.tile([P, I // PER_COLUMN], U16, name=name)
+            nc.sync.dma_start(tile[:], source)
+            return tile
+
+        q_raw = sb.tile([P, PACK, Q], F32, name="q_raw", align_bytes=64)
+        key_words = sb.tile([P, 2 * T], U8, name="key_words", align_bytes=64)
+        note_words = sb.tile([P, U], U32, name="note_words", align_bytes=64)
+        nc.sync.dma_start(out=q_raw[:], in_=query.rearrange("(p j) q -> p j q", j=PACK))
+        for quadrant in range(4):
+            load_scales(nc.sync, key_plane, keys_scales, quadrant)
+        nc.sync.dma_start(out=key_words[:].bitcast(I32), in_=keys_words[0].bitcast(I32))
+        nc.sync.dma_start(
+            out=note_words[:].bitcast(I32), in_=notes_words[0].rearrange("p n t -> p (n t)").bitcast(I32)
+        )
+        for quadrant in range(4):
+            load_scales(nc.sync, note_plane, notes_scales, quadrant)
+        idx = load_list("idx", offs)
+        idx2 = load_list("idx2", offs2)
+        idx3 = load_list("idx3", offs3)
+        idx4 = load_list("idx4", offs4)
+        idx5 = load_list("idx5", offs5)
+
+        q_grouped = sb.tile([P, Q, PACK], BF16, name="q_grouped", align_bytes=64)
+        nc.vector.tensor_copy(
+            out=q_grouped[:].rearrange("p (c i) j -> p c j i", i=4),
+            in_=q_raw[:].rearrange("p j (c i) -> p c j i", i=4),
+        )
+        q_words = sb.tile([P, Q], U32, name="q_words", align_bytes=64)
+        q_plane = sb.tile([P, Q], U8, name="q_plane", align_bytes=64)
+        nc.vector.quantize_mx(
+            out=q_words[:].bitcast(FP8X4), scales=q_plane[:], in_=q_grouped[:].rearrange("p q j -> p (q j)")
+        )
+
+        def score(name, words, plane):
+            bank = psum.tile([P, N], F32, name=name)
+            nc.tensor.matmul_mx(
+                out=bank[:],
+                lhsT=q_words[:].bitcast(FP8X4),
+                lhsT_scale=q_plane[:],
+                rhs=words,
+                rhs_scale=plane,
+                start=True,
+                stop=True,
+            )
+            return bank
+
+        a_banks = [
+            score("a_bank%d" % c, key_words[:, 2 * N * c : 2 * N * (c + 1)].bitcast(FP4X4), key_plane[:, N * c : N * (c + 1)])
+            for c in range(T // N)
+        ]
+        b_banks = [
+            score("b_bank%d" % c, note_words[:, N * c : N * (c + 1)].bitcast(FP8X4), note_plane[:, N * c : N * (c + 1)])
+            for c in range(U // N)
+        ]
+
+        a = sb.tile([P, T], F32, name="a", align_bytes=64)
+        b = sb.tile([P, U], F32, name="b", align_bytes=64)
+        for c, bank in enumerate(a_banks):
+            if c % 2 == 1:
+                nc.vector.tensor_copy(out=a[:, N * c : N * (c + 1)], in_=bank[:])
+            else:
+                nc.scalar.activation(a[:, N * c : N * (c + 1)], bank[:], COPY)
+        for c, bank in enumerate(b_banks):
+            nc.scalar.activation(b[:, N * c : N * (c + 1)], bank[:], COPY)
+
+        def slots(h):
+            return slice(HALF * h, HALF * (h + 1))
+
+        def entries(tile, h):
+            return tile[:, HALF // PER_COLUMN * h : HALF // PER_COLUMN * (h + 1)]
+
+        looked = [sb.tile([P, I], F32, name="looked%d" % h, align_bytes=64) for h in range(2)]
+        a_first = [looked[h][:, 0:HALF] for h in range(2)]
+        a_second = [looked[h][:, HALF:I] for h in range(2)]
+        b_late = sb.tile([P, HALF], F32, name="b_late", align_bytes=64)
+        b_third = [looked[1][:, HALF // 2 : HALF // 2 + HALF], b_late[:]]
+        w = sb.tile([P, I], F32, name="w", align_bytes=64)
+        v = sb.tile([P, I], F32, name="v", align_bytes=64)
+
+        def lower_and_place(h):
+            nc.vector.tensor_tensor(w[:, slots(h)], a_first[h], a_second[h], ALU.min)
+            nc.vector.tensor_tensor(v[:, slots(h)], w[:, slots(h)], b_third[h], ALU.min)
+            nc.vector.tensor_copy(f1[:].indirect(entries(idx4, h)), v[:, slots(h)])
+
+        nc.vector.tensor_copy(a_first[0], a[:].indirect(entries(idx, 0)))
+        nc.vector.tensor_copy(a_second[0], a[:].indirect(entries(idx2, 0)))
+        for h in range(2):
+            nc.scalar.activation(b_third[h], b[:].indirect(entries(idx3, h)), COPY)
+        lower_and_place(0)
+        nc.scalar.activation(a_first[1], a[:].indirect(entries(idx, 1)), COPY)
+        nc.scalar.activation(a_second[1], a[:].indirect(entries(idx2, 1)), COPY)
+        lower_and_place(1)
+
+        bb = sb.tile([P, U], F32, name="bb", align_bytes=64)
+        nc.vector.tensor_tensor(bb[:], b[:], f1[:], ALU.subtract)
+        result = sb.tile([P, I], F32, name="result", align_bytes=64)
+        left = sb.tile([P, HALF], F32, name="left", align_bytes=64)
+        nc.vector.tensor_tensor(result[:, slots(0)], bb[:].indirect(entries(idx5, 0)), w[:, slots(0)], ALU.add)
+        nc.scalar.activation(left[:], bb[:].indirect(entries(idx5, 1)), COPY)
+        nc.sync.dma_start(out=out[:, slots(0)], in_=result[:, slots(0)])
+        nc.vector.tensor_tensor(result[:, slots(1)], left[:], w[:, slots(1)], ALU.add)
+        nc.sync.dma_start(out=out[:, slots(1)], in_=result[:, slots(1)])

@@ -18,9 +18,12 @@ COPY = mybir.ActivationFunctionType.Copy
 
 P = 128
 PACK = 4
-N = 256
 HALF = I // 2
 PER_COLUMN = 16
+Q_VECTOR = 88
+BANKS = 8
+NOTE_ROW = 4
+PASSES = [slice(0, 256), slice(256, 512), slice(512, 768), slice(768, 896), slice(896, 1024)]
 
 
 def tile_attend_weakestlink_two_kernel(
@@ -40,9 +43,10 @@ def tile_attend_weakestlink_two_kernel(
         nc.vector.memset(note_plane[:].bitcast(I32), 0)
         nc.vector.memset(f1[:], 0.0)
 
-        def load_scales(queue, plane, scales, quadrant):
-            queue.dma_start(
-                out=plane[32 * quadrant : 32 * quadrant + 4, :].bitcast(I32),
+        def load_scales(plane, first_row, scales, quadrant):
+            row = 32 * quadrant + first_row
+            nc.sync.dma_start(
+                out=plane[row : row + 4, :].bitcast(I32),
                 in_=scales[0, 4 * quadrant : 4 * quadrant + 4, :].bitcast(I32),
             )
 
@@ -55,33 +59,36 @@ def tile_attend_weakestlink_two_kernel(
         key_words = sb.tile([P, 2 * T], U8, name="key_words", align_bytes=64)
         note_words = sb.tile([P, U], U32, name="note_words", align_bytes=64)
         nc.sync.dma_start(out=q_raw[:], in_=query.rearrange("(p j) q -> p j q", j=PACK))
-        for quadrant in range(4):
-            load_scales(nc.sync, key_plane, keys_scales, quadrant)
+        for quadrant in range(2):
+            load_scales(key_plane, 0, keys_scales, quadrant)
         nc.sync.dma_start(out=key_words[:].bitcast(I32), in_=keys_words[0].bitcast(I32))
+        for quadrant in range(2, 4):
+            load_scales(key_plane, 0, keys_scales, quadrant)
         nc.sync.dma_start(
             out=note_words[:].bitcast(I32), in_=notes_words[0].rearrange("p n t -> p (n t)").bitcast(I32)
         )
         for quadrant in range(4):
-            load_scales(nc.sync, note_plane, notes_scales, quadrant)
-        idx = load_list("idx", offs)
+            load_scales(note_plane, NOTE_ROW, notes_scales, quadrant)
         idx2 = load_list("idx2", offs2)
+        idx = load_list("idx", offs)
         idx3 = load_list("idx3", offs3)
         idx4 = load_list("idx4", offs4)
         idx5 = load_list("idx5", offs5)
 
         q_grouped = sb.tile([P, Q, PACK], BF16, name="q_grouped", align_bytes=64)
-        nc.vector.tensor_copy(
-            out=q_grouped[:].rearrange("p (c i) j -> p c j i", i=4),
-            in_=q_raw[:].rearrange("p j (c i) -> p c j i", i=4),
-        )
+        for rows, copy in ((slice(0, Q_VECTOR), nc.vector.tensor_copy), (slice(Q_VECTOR, Q), nc.scalar.copy)):
+            copy(
+                out=q_grouped[:, rows, :].rearrange("p (c i) j -> p c j i", i=4),
+                in_=q_raw[:, :, rows].rearrange("p j (c i) -> p c j i", i=4),
+            )
         q_words = sb.tile([P, Q], U32, name="q_words", align_bytes=64)
         q_plane = sb.tile([P, Q], U8, name="q_plane", align_bytes=64)
         nc.vector.quantize_mx(
             out=q_words[:].bitcast(FP8X4), scales=q_plane[:], in_=q_grouped[:].rearrange("p q j -> p (q j)")
         )
 
-        def score(name, words, plane):
-            bank = psum.tile([P, N], F32, name=name)
+        def score(bank_name, cols, words, plane):
+            bank = psum.tile([P, cols.stop - cols.start], F32, name=bank_name)
             nc.tensor.matmul_mx(
                 out=bank[:],
                 lhsT=q_words[:].bitcast(FP8X4),
@@ -93,24 +100,19 @@ def tile_attend_weakestlink_two_kernel(
             )
             return bank
 
-        a_banks = [
-            score("a_bank%d" % c, key_words[:, 2 * N * c : 2 * N * (c + 1)].bitcast(FP4X4), key_plane[:, N * c : N * (c + 1)])
-            for c in range(T // N)
-        ]
-        b_banks = [
-            score("b_bank%d" % c, note_words[:, N * c : N * (c + 1)].bitcast(FP8X4), note_plane[:, N * c : N * (c + 1)])
-            for c in range(U // N)
-        ]
-
         a = sb.tile([P, T], F32, name="a", align_bytes=64)
         b = sb.tile([P, U], F32, name="b", align_bytes=64)
-        for c, bank in enumerate(a_banks):
-            if c % 2 == 1:
-                nc.vector.tensor_copy(out=a[:, N * c : N * (c + 1)], in_=bank[:])
+        for c, cols in enumerate(PASSES):
+            words = key_words[:, 2 * cols.start : 2 * cols.stop].bitcast(FP4X4)
+            bank = score("bank%d" % c, cols, words, key_plane[:, cols])
+            if c in (1, 4):
+                nc.vector.tensor_copy(out=a[:, cols], in_=bank[:])
             else:
-                nc.scalar.activation(a[:, N * c : N * (c + 1)], bank[:], COPY)
-        for c, bank in enumerate(b_banks):
-            nc.scalar.activation(b[:, N * c : N * (c + 1)], bank[:], COPY)
+                nc.scalar.activation(a[:, cols], bank[:], COPY)
+        for c, cols in enumerate(PASSES):
+            words = note_words[:, cols].bitcast(FP8X4)
+            bank = score("bank%d" % ((len(PASSES) + c) % BANKS), cols, words, note_plane[NOTE_ROW:P, cols])
+            nc.scalar.activation(b[:, cols], bank[:], COPY)
 
         def slots(h):
             return slice(HALF * h, HALF * (h + 1))
@@ -118,27 +120,32 @@ def tile_attend_weakestlink_two_kernel(
         def entries(tile, h):
             return tile[:, HALF // PER_COLUMN * h : HALF // PER_COLUMN * (h + 1)]
 
-        looked = [sb.tile([P, I], F32, name="looked%d" % h, align_bytes=64) for h in range(2)]
-        a_first = [looked[h][:, 0:HALF] for h in range(2)]
-        a_second = [looked[h][:, HALF:I] for h in range(2)]
-        b_late = sb.tile([P, HALF], F32, name="b_late", align_bytes=64)
-        b_third = [looked[1][:, HALF // 2 : HALF // 2 + HALF], b_late[:]]
+        a_first = sb.tile([P, I], F32, name="a_first", align_bytes=64)
+        early = sb.tile([P, HALF], F32, name="early", align_bytes=64)
+        reused = sb.tile([P, HALF], F32, name="reused", align_bytes=64)
+        late = sb.tile([P, HALF], F32, name="late", align_bytes=64)
+        a_second = [early[:], reused[:]]
+        b_third = [reused[:], late[:]]
+        partial = sb.tile([P, HALF], F32, name="partial", align_bytes=64)
         w = sb.tile([P, I], F32, name="w", align_bytes=64)
         v = sb.tile([P, I], F32, name="v", align_bytes=64)
 
-        def lower_and_place(h):
-            nc.vector.tensor_tensor(w[:, slots(h)], a_first[h], a_second[h], ALU.min)
-            nc.vector.tensor_tensor(v[:, slots(h)], w[:, slots(h)], b_third[h], ALU.min)
+        def place(h):
             nc.vector.tensor_copy(f1[:].indirect(entries(idx4, h)), v[:, slots(h)])
 
-        nc.vector.tensor_copy(a_first[0], a[:].indirect(entries(idx, 0)))
         nc.vector.tensor_copy(a_second[0], a[:].indirect(entries(idx2, 0)))
         for h in range(2):
+            nc.vector.tensor_copy(a_first[:, slots(h)], a[:].indirect(entries(idx, h)))
+        for h in range(2):
             nc.scalar.activation(b_third[h], b[:].indirect(entries(idx3, h)), COPY)
-        lower_and_place(0)
-        nc.scalar.activation(a_first[1], a[:].indirect(entries(idx, 1)), COPY)
+        nc.vector.tensor_tensor(w[:, slots(0)], a_first[:, slots(0)], a_second[0], ALU.min)
+        nc.vector.tensor_tensor(v[:, slots(0)], w[:, slots(0)], b_third[0], ALU.min)
         nc.scalar.activation(a_second[1], a[:].indirect(entries(idx2, 1)), COPY)
-        lower_and_place(1)
+        nc.vector.tensor_tensor(partial[:], a_first[:, slots(1)], b_third[1], ALU.min)
+        place(0)
+        nc.vector.tensor_tensor(v[:, slots(1)], partial[:], a_second[1], ALU.min)
+        nc.vector.tensor_tensor(w[:, slots(1)], a_first[:, slots(1)], a_second[1], ALU.min)
+        place(1)
 
         bb = sb.tile([P, U], F32, name="bb", align_bytes=64)
         nc.vector.tensor_tensor(bb[:], b[:], f1[:], ALU.subtract)

@@ -22,6 +22,7 @@ HALF = I // 2
 PER_COLUMN = 16
 Q_VECTOR = 88
 BANKS = 8
+U_VECTOR = 832
 NOTE_ROW = 4
 PASSES = [slice(0, 256), slice(256, 512), slice(512, 768), slice(768, 896), slice(896, 1024)]
 
@@ -38,8 +39,7 @@ def tile_attend_weakestlink_two_kernel(
         key_plane = sb.tile([P, T], U8, name="key_plane", align_bytes=64)
         note_plane = sb.tile([P, U], U8, name="note_plane", align_bytes=64)
         f1 = sb.tile([P, U], F32, name="f1", align_bytes=64)
-        nc.vector.memset(key_plane[:, 0 : T // 2].bitcast(I32), 0)
-        nc.gpsimd.memset(key_plane[:, T // 2 : T].bitcast(I32), 0)
+        nc.vector.memset(key_plane[:].bitcast(I32), 0)
         nc.vector.memset(note_plane[:].bitcast(I32), 0)
         nc.vector.memset(f1[:], 0.0)
 
@@ -109,10 +109,12 @@ def tile_attend_weakestlink_two_kernel(
                 nc.vector.tensor_copy(out=a[:, cols], in_=bank[:])
             else:
                 nc.scalar.activation(a[:, cols], bank[:], COPY)
+        b_banks = []
         for c, cols in enumerate(PASSES):
             words = note_words[:, cols].bitcast(FP8X4)
             bank = score("bank%d" % ((len(PASSES) + c) % BANKS), cols, words, note_plane[NOTE_ROW:P, cols])
             nc.scalar.activation(b[:, cols], bank[:], COPY)
+            b_banks.append(bank)
 
         def slots(h):
             return slice(HALF * h, HALF * (h + 1))
@@ -148,7 +150,12 @@ def tile_attend_weakestlink_two_kernel(
         place(1)
 
         bb = sb.tile([P, U], F32, name="bb", align_bytes=64)
-        nc.vector.tensor_tensor(bb[:], b[:], f1[:], ALU.subtract)
+        for cols, bank in zip(PASSES[:4], b_banks):
+            stop = min(cols.stop, U_VECTOR)
+            nc.vector.tensor_tensor(
+                bb[:, cols.start : stop], bank[:, 0 : stop - cols.start], f1[:, cols.start : stop], ALU.subtract
+            )
+        nc.gpsimd.tensor_tensor(bb[:, U_VECTOR:U], b[:, U_VECTOR:U], f1[:, U_VECTOR:U], ALU.subtract)
         result = sb.tile([P, I], F32, name="result", align_bytes=64)
         left = sb.tile([P, HALF], F32, name="left", align_bytes=64)
         nc.vector.tensor_tensor(result[:, slots(0)], bb[:].indirect(entries(idx5, 0)), w[:, slots(0)], ALU.add)

from contextlib import ExitStack

import concourse.mybir as mybir

D, T, U, I, Q = 512, 1024, 1024, 512, 128
FLOPS = 2 * D * Q * (T + U)

F32 = mybir.dt.float32
BF16 = mybir.dt.bfloat16
I32 = mybir.dt.int32
U32 = mybir.dt.uint32
U16 = mybir.dt.uint16
U8 = mybir.dt.uint8
FP8X4 = mybir.dt.float8_e4m3fn_x4
FP4X4 = mybir.dt.float4_e2m1fn_x4
ALU = mybir.AluOpType
COPY = mybir.ActivationFunctionType.Copy

P = 128
PACK = 4
HALF = I // 2
PER_COLUMN = 16
Q_VECTOR = 88
BANKS = 8
U_VECTOR = 832
NOTE_ROW = 4
PASSES = [slice(0, 256), slice(256, 512), slice(512, 768), slice(768, 896), slice(896, 1024)]


def tile_attend_weakestlink_two_kernel(
    tc, query, keys_words, keys_scales, notes_words, notes_scales, offs, offs2, offs3, offs4, offs5, out
):
    nc = tc.nc
    with ExitStack() as ctx:
        lists = ctx.enter_context(tc.tile_pool(name="lists", bufs=1))
        sb = ctx.enter_context(tc.tile_pool(name="sb", bufs=1))
        psum = ctx.enter_context(tc.psum_pool(name="psum", bufs=1))

        key_plane = sb.tile([P, T], U8, name="key_plane", align_bytes=64)
        note_plane = sb.tile([P, U], U8, name="note_plane", align_bytes=64)
        f1 = sb.tile([P, U], F32, name="f1", align_bytes=64)
        nc.vector.memset(key_plane[:].bitcast(I32), 0)
        nc.vector.memset(note_plane[:].bitcast(I32), 0)
        nc.vector.memset(f1[:], 0.0)

        def load_scales(plane, first_row, scales, quadrant):
            row = 32 * quadrant + first_row
            nc.sync.dma_start(
                out=plane[row : row + 4, :].bitcast(I32),
                in_=scales[0, 4 * quadrant : 4 * quadrant + 4, :].bitcast(I32),
            )

        def load_list(name, source):
            tile = lists.tile([P, I // PER_COLUMN], U16, name=name)
            nc.sync.dma_start(tile[:], source)
            return tile

        q_raw = sb.tile([P, PACK, Q], F32, name="q_raw", align_bytes=64)
        key_words = sb.tile([P, 2 * T], U8, name="key_words", align_bytes=64)
        note_words = sb.tile([P, U], U32, name="note_words", align_bytes=64)
        nc.sync.dma_start(out=q_raw[:], in_=query.rearrange("(p j) q -> p j q", j=PACK))
        for quadrant in range(2):
            load_scales(key_plane, 0, keys_scales, quadrant)
        nc.sync.dma_start(out=key_words[:].bitcast(I32), in_=keys_words[0].bitcast(I32))
        for quadrant in range(2, 4):
            load_scales(key_plane, 0, keys_scales, quadrant)
        nc.sync.dma_start(
            out=note_words[:].bitcast(I32), in_=notes_words[0].rearrange("p n t -> p (n t)").bitcast(I32)
        )
        for quadrant in range(4):
            load_scales(note_plane, NOTE_ROW, notes_scales, quadrant)
        idx2 = load_list("idx2", offs2)
        idx = load_list("idx", offs)
        idx3 = load_list("idx3", offs3)
        idx4 = load_list("idx4", offs4)
        idx5 = load_list("idx5", offs5)

        q_grouped = sb.tile([P, Q, PACK], BF16, name="q_grouped", align_bytes=64)
        for rows, copy in ((slice(0, Q_VECTOR), nc.vector.tensor_copy), (slice(Q_VECTOR, Q), nc.scalar.copy)):
            copy(
                out=q_grouped[:, rows, :].rearrange("p (c i) j -> p c j i", i=4),
                in_=q_raw[:, :, rows].rearrange("p j (c i) -> p c j i", i=4),
            )
        q_words = sb.tile([P, Q], U32, name="q_words", align_bytes=64)
        q_plane = sb.tile([P, Q], U8, name="q_plane", align_bytes=64)
        nc.vector.quantize_mx(
            out=q_words[:].bitcast(FP8X4), scales=q_plane[:], in_=q_grouped[:].rearrange("p q j -> p (q j)")
        )

        def score(bank_name, cols, words, plane):
            bank = psum.tile([P, cols.stop - cols.start], F32, name=bank_name)
            nc.tensor.matmul_mx(
                out=bank[:],
                lhsT=q_words[:].bitcast(FP8X4),
                lhsT_scale=q_plane[:],
                rhs=words,
                rhs_scale=plane,
                start=True,
                stop=True,
            )
            return bank

        a = sb.tile([P, T], F32, name="a", align_bytes=64)
        b = sb.tile([P, U], F32, name="b", align_bytes=64)
        for c, cols in enumerate(PASSES):
            words = key_words[:, 2 * cols.start : 2 * cols.stop].bitcast(FP4X4)
            bank = score("bank%d" % c, cols, words, key_plane[:, cols])
            if c in (1, 4):
                nc.vector.tensor_copy(out=a[:, cols], in_=bank[:])
            else:
                nc.scalar.activation(a[:, cols], bank[:], COPY)
        b_banks = []
        for c, cols in enumerate(PASSES):
            words = note_words[:, cols].bitcast(FP8X4)
            bank = score("bank%d" % ((len(PASSES) + c) % BANKS), cols, words, note_plane[NOTE_ROW:P, cols])
            nc.scalar.activation(b[:, cols], bank[:], COPY)
            b_banks.append(bank)

        def slots(h):
            return slice(HALF * h, HALF * (h + 1))

        def entries(tile, h):
            return tile[:, HALF // PER_COLUMN * h : HALF // PER_COLUMN * (h + 1)]

        a_first = sb.tile([P, I], F32, name="a_first", align_bytes=64)
        early = sb.tile([P, HALF], F32, name="early", align_bytes=64)
        reused = sb.tile([P, HALF], F32, name="reused", align_bytes=64)
        late = sb.tile([P, HALF], F32, name="late", align_bytes=64)
        a_second = [early[:], reused[:]]
        b_third = [reused[:], late[:]]
        partial = sb.tile([P, HALF], F32, name="partial", align_bytes=64)
        w = sb.tile([P, I], F32, name="w", align_bytes=64)
        v = sb.tile([P, I], F32, name="v", align_bytes=64)

        def place(h):
            nc.vector.tensor_copy(f1[:].indirect(entries(idx4, h)), v[:, slots(h)])

        nc.vector.tensor_copy(a_second[0], a[:].indirect(entries(idx2, 0)))
        for h in range(2):
            nc.vector.tensor_copy(a_first[:, slots(h)], a[:].indirect(entries(idx, h)))
        for h in range(2):
            nc.scalar.activation(b_third[h], b[:].indirect(entries(idx3, h)), COPY)
        nc.vector.tensor_tensor(w[:, slots(0)], a_first[:, slots(0)], a_second[0], ALU.min)
        nc.vector.tensor_tensor(v[:, slots(0)], w[:, slots(0)], b_third[0], ALU.min)
        nc.scalar.activation(a_second[1], a[:].indirect(entries(idx2, 1)), COPY)
        nc.vector.tensor_tensor(partial[:], a_first[:, slots(1)], b_third[1], ALU.min)
        place(0)
        nc.vector.tensor_tensor(v[:, slots(1)], partial[:], a_second[1], ALU.min)
        nc.vector.tensor_tensor(w[:, slots(1)], a_first[:, slots(1)], a_second[1], ALU.min)
        place(1)

        bb = sb.tile([P, U], F32, name="bb", align_bytes=64)
        for cols, bank in zip(PASSES[:4], b_banks):
            stop = min(cols.stop, U_VECTOR)
            nc.vector.tensor_tensor(
                bb[:, cols.start : stop], bank[:, 0 : stop - cols.start], f1[:, cols.start : stop], ALU.subtract
            )
        nc.gpsimd.tensor_tensor(bb[:, U_VECTOR:U], b[:, U_VECTOR:U], f1[:, U_VECTOR:U], ALU.subtract)
        result = sb.tile([P, I], F32, name="result", align_bytes=64)
        left = sb.tile([P, HALF], F32, name="left", align_bytes=64)
        nc.vector.tensor_tensor(result[:, slots(0)], bb[:].indirect(entries(idx5, 0)), w[:, slots(0)], ALU.add)
        nc.scalar.activation(left[:], bb[:].indirect(entries(idx5, 1)), COPY)
        nc.sync.dma_start(out=out[:, slots(0)], in_=result[:, slots(0)])
        nc.vector.tensor_tensor(result[:, slots(1)], left[:], w[:, slots(1)], ALU.add)
        nc.sync.dma_start(out=out[:, slots(1)], in_=result[:, slots(1)])
